import numpy as np
import ml_dtypes


def mxq(x, axis, fmt="e4m3"):
    dtype, down = {"e4m3": (ml_dtypes.float8_e4m3fn, 7), "e5m2": (ml_dtypes.float8_e5m2, 14)}[fmt]
    v = np.moveaxis(np.asarray(x, np.float32).astype(ml_dtypes.bfloat16).astype(np.float64), axis, -1)
    blocks = v.reshape(v.shape[:-1] + (-1, 32))
    amax = np.abs(blocks).max(-1, keepdims=True)
    byte = np.maximum(np.where(amax > 0, np.frexp(amax)[1] - 1 + 127, 0) - down, 1)
    scale = np.exp2(byte - 127.0)
    codes = (blocks / scale).astype(np.float32).astype(dtype).astype(np.float64)
    return np.moveaxis((codes * scale).reshape(v.shape), -1, axis)


WIDE = False


def mx_kscale(k):
    if not WIDE:
        return np.ones(k)
    levels = np.array([10, -10, 5, -5, 0])
    if k % 512:
        return np.exp2(np.random.permutation(np.resize(levels, k // 32))).repeat(32)
    a = np.empty((k // 512, 16))
    for p in range(k // 512):
        a[p, :8] = np.random.permutation(np.resize(levels, 8))
        for g in range(8):
            far = levels[np.abs(levels - a[p, g]) >= 10]
            a[p, g + 8] = far[np.random.randint(len(far))]
    return np.exp2(a.ravel()).repeat(32)


def f64(x):
    return np.asarray(x).astype(np.float64)


def striped(idx):
    return np.tile(idx.reshape(-1, 16).T, (8, 1)).astype(np.uint16)


def unstriped(offs):
    return offs[:16].T.reshape(-1).astype(np.int64)


E2M1 = np.array([0.0, 0.5, 1.0, 1.5, 2.0, 3.0, 4.0, 6.0, -0.0, -0.5, -1.0, -1.5, -2.0, -3.0, -4.0, -6.0])


def pack_fp4(w):
    k, n = w.shape
    w = f64(np.asarray(w, np.float32).astype(ml_dtypes.bfloat16)).reshape(k // 32, 32, n)
    amax = np.abs(w).max(1)
    mant, ex = np.frexp(amax / 6.0)
    byte = np.clip(np.where(amax > 0, np.where(mant > 0.5, ex, ex - 1) + 127, 1), 1, 254)
    scaled = (w * np.exp2(127.0 - byte)[:, None, :]).reshape(k, n).astype(np.float32)
    c = np.ascontiguousarray(scaled.reshape(k // 512, 128, 4, n).transpose(0, 1, 3, 2)).astype(ml_dtypes.float4_e2m1fn).view(np.uint8) & 0xF
    words = (c[..., 0::2] | (c[..., 1::2] << 4)).reshape(k // 512, 128, 2 * n)
    return np.ascontiguousarray(words), np.ascontiguousarray(byte.astype(np.uint8).reshape(k // 512, 16, n))


def unpack_fp4(words, scales):
    g, _, n = scales.shape
    words = np.ascontiguousarray(words).reshape(g, 128, n, 2)
    nib = np.empty((g, 128, n, 4), np.uint8)
    nib[..., 0::2] = words & 0xF
    nib[..., 1::2] = words >> 4
    vals = E2M1[nib] * np.repeat(np.exp2(scales.astype(np.float64) - 127.0), 8, axis=1)[..., None]
    return vals.transpose(0, 1, 3, 2).reshape(g * 512, n)


def relu(v):
    return np.maximum(v, 0.0)


K, T, S, D, V, H, N, U = 512, 2048, 512, 2, 512, 512, 256, 1024
P = 2 ** 7


def setup_inputs():
    n = np.random.standard_normal
    s = mx_kscale(K)[:, None]
    u = mx_kscale(H)
    packed_w2 = pack_fp4(n((H, N)) / np.sqrt(H) / u[:, None])
    return {
        "xT": (n((K, T)) * s).astype(np.float32),
        "w1": (n((K, H)) / np.sqrt(K) / s * u).astype(np.float32),
        "w2_words": packed_w2[0],
        "w2_scales": packed_w2[1],
        "gate": np.tile(np.random.uniform(0.2, 0.6, (D, 1, V)), (1, P, 1)).astype(np.float32),
        "emb": (0.5 * n((H, U)) * u[:, None]).astype(np.float32),
        "offs": striped(np.random.permutation(T)[:S]),
        "cell": striped(np.random.permutation(U)[:S]),
        "pos1": striped(np.random.permutation(U)[:V]),
        "pos2": striped(np.random.permutation(U)[:V]),
    }


def reference(xT, w1, w2_words, w2_scales, gate, emb, offs, cell, pos1, pos2):
    xq = mxq(f64(xT)[:, unstriped(offs)], 0, "e4m3")
    up = np.zeros((H, U))
    up[:, unstriped(cell)] = relu(mxq(f64(w1), 0, "e4m3").T @ xq)
    z = up + f64(emb)
    y = relu(unpack_fp4(w2_words, w2_scales).T @ mxq(z, 0, "e4m3"))
    return y[:, unstriped(pos1)] * f64(gate)[0, :1] + y[:, unstriped(pos2)] * f64(gate)[1, :1]

@@ -1,0 +1,219 @@
+from contextlib import ExitStack
+
+import concourse.mybir as mybir
+
+K, T, S, V, H, N, U = 512, 2048, 512, 512, 512, 256, 1024
+FLOPS = 2 * K * H * S + 2 * H * N * U
+
+F32 = mybir.dt.float32
+BF16 = mybir.dt.bfloat16
+I32 = mybir.dt.int32
+U32 = mybir.dt.uint32
+U16 = mybir.dt.uint16
+U8 = mybir.dt.uint8
+FP8X4 = mybir.dt.float8_e4m3fn_x4
+FP4X4 = mybir.dt.float4_e2m1fn_x4
+ADD = mybir.AluOpType.add
+MULT = mybir.AluOpType.mult
+RELU = mybir.ActivationFunctionType.Relu
+COPY = mybir.ActivationFunctionType.Copy
+
+P = 128
+PACK = 4
+LIST_ROWS = 16
+HALF = 256
+CHUNK = 256
+CHUNKS = U // CHUNK
+SLOT_ORDER = (2, 0, 1, 3)
+
+
+def tile_picked_devox_relu_e_kernel(
+    tc, xT, w1, w2_words, w2_scales, gate, emb, offs, cell, pos1, pos2, out
+):
+    nc = tc.nc
+    with ExitStack() as ctx:
+        keep = ctx.enter_context(tc.tile_pool(name="keep", bufs=1))
+        psum = ctx.enter_context(tc.psum_pool(name="psum", bufs=1))
+
+        def load_list(src, name):
+            tile = keep.tile([P, src.shape[1]], U16, name=name)
+            nc.sync.dma_start(tile[:], src)
+            return tile
+
+        def entries(lst, first, count):
+            return lst[:, first // LIST_ROWS : (first + count) // LIST_ROWS]
+
+        def bank(index, width, name):
+            return psum.tile([P, width], F32, name=name, tag="bank%d" % index)
+
+        offs_sb = load_list(offs, "offs_sb")
+        w1_raw = keep.tile([P, PACK, H], F32, name="w1_raw")
+        nc.sync.dma_start(w1_raw[:], w1.rearrange("(p j) c -> p j c", j=PACK))
+        x_rows = xT.rearrange("(p j) t -> p j t", j=PACK)
+        x_plane = []
+        for j in range(PACK):
+            plane = keep.tile([P, T], F32, name="x_plane%d" % j)
+            nc.sync.dma_start(plane[:], x_rows[:, j, :])
+            x_plane.append(plane)
+        cell_sb = load_list(cell, "cell_sb")
+        emb_rows = emb.rearrange("(p t) r -> p t r", t=PACK)
+        emb_sb = {}
+        for t in SLOT_ORDER:
+            emb_sb[t] = keep.tile([P, U], F32, name="emb%d" % t)
+            nc.sync.dma_start(emb_sb[t][:], emb_rows[:, t, :])
+        w2_codes = keep.tile([P, 2 * N], U8, name="w2_codes", align_bytes=64)
+        nc.sync.dma_start(w2_codes[:].bitcast(I32), w2_words[0].bitcast(I32))
+        pos_sb = [load_list(pos1, "pos1_sb"), load_list(pos2, "pos2_sb")]
+        gate_sb = []
+        for d in range(2):
+            g = keep.tile([P, V], F32, name="gate%d" % d)
+            nc.sync.dma_start(g[:], gate[d])
+            gate_sb.append(g)
+        w2_plane = keep.tile([P, N], U8, name="w2_plane", align_bytes=64)
+        nc.gpsimd.memset(w2_plane[:], 0)
+        for q in range(4):
+            nc.sync.dma_start(
+                w2_plane[32 * q : 32 * q + 4, :].bitcast(I32), w2_scales[0, 4 * q : 4 * q + 4, :].bitcast(I32)
+            )
+
+        def cleared_window(t, tag):
+            window = keep.tile([P, U], F32, name="up%d" % t, tag=tag)
+            nc.gpsimd.memset(window[:], 0.0)
+            return window
+
+        up = {t: cleared_window(t, "up%d" % t) for t in SLOT_ORDER[:3]}
+
+        w1_grouped = keep.tile([P, PACK, P, PACK], BF16, name="w1_grouped", align_bytes=64)
+        nc.scalar.activation(
+            w1_grouped[:].rearrange("p t m j -> p m t j"), w1_raw[:].rearrange("p j (m t) -> p m t j", t=PACK), COPY
+        )
+        w1_codes = keep.tile([P, H], U32, name="w1_codes", align_bytes=64)
+        w1_plane = keep.tile([P, H], U8, name="w1_plane", align_bytes=64)
+        nc.vector.quantize_mx(
+            out=w1_codes[:].bitcast(FP8X4), scales=w1_plane[:], in_=w1_grouped[:].rearrange("p t m j -> p (t m j)")
+        )
+
+        x_grouped = keep.tile([P, S, PACK], BF16, name="x_grouped", align_bytes=64)
+        x_codes = keep.tile([P, S], U32, name="x_codes", align_bytes=64)
+        x_scales = keep.tile([P, S], U8, name="x_scales", align_bytes=64)
+        for j in range(PACK - 1):
+            nc.vector.tensor_copy(x_grouped[:, :, j], x_plane[j][:].indirect(offs_sb[:]))
+        for first in range(0, S, HALF):
+            nc.vector.tensor_copy(
+                x_grouped[:, first : first + HALF, PACK - 1],
+                x_plane[PACK - 1][:].indirect(entries(offs_sb, first, HALF)),
+            )
+        for first in range(0, S, HALF):
+            cols = slice(first, first + HALF)
+            nc.vector.quantize_mx(
+                out=x_codes[:, cols].bitcast(FP8X4),
+                scales=x_scales[:, cols],
+                in_=x_grouped[:, cols, :].rearrange("p s j -> p (s j)"),
+            )
+
+        pairs = keep.tile([P, CHUNKS, 2, CHUNK, 2], BF16, name="pairs", align_bytes=64)
+
+        def first_product(t, first, count, bank_index):
+            cols = slice(first, first + count)
+            rows = slice(P * t, P * (t + 1))
+            acc = bank(bank_index, count, "h_acc%d_%d" % (t, first))
+            nc.tensor.matmul_mx(
+                out=acc[:],
+                lhsT=w1_codes[:, rows].bitcast(FP8X4),
+                lhsT_scale=w1_plane[:, rows],
+                rhs=x_codes[:, cols].bitcast(FP8X4),
+                rhs_scale=x_scales[:, cols],
+                start=True,
+                stop=True,
+            )
+            h = keep.tile([P, count], F32, name="h%d_%d" % (t, first))
+            nc.scalar.activation(h[:], acc[:], RELU)
+            return h
+
+        def scatter(t, h, first, count):
+            nc.vector.tensor_copy(up[t][:].indirect(entries(cell_sb, first, count)), h[:])
+
+        def add_emb_whole(t):
+            nc.gpsimd.tensor_tensor(
+                pairs[:, :, t // 2, :, t % 2],
+                up[t][:].rearrange("p (c r) -> p c r", r=CHUNK),
+                emb_sb[t][:].rearrange("p (c r) -> p c r", r=CHUNK),
+                ADD,
+            )
+
+        lead = SLOT_ORDER[0]
+        lead_halves = [first_product(lead, first, HALF, first // HALF) for first in range(0, S, HALF)]
+        h_rest = {t: first_product(t, 0, S, 2 + i) for i, t in enumerate(SLOT_ORDER[1:])}
+        for i, h in enumerate(lead_halves):
+            scatter(lead, h, i * HALF, HALF)
+        add_emb_whole(lead)
+        last = SLOT_ORDER[3]
+        up[last] = cleared_window(last, "up%d" % lead)
+        for t in SLOT_ORDER[1:3]:
+            scatter(t, h_rest[t], 0, S)
+            add_emb_whole(t)
+        scatter(last, h_rest[last], 0, S)
+
+        y = [keep.tile([P, U], F32, name="y%d" % m) for m in range(N // P)]
+        z_codes, z_scales = [], []
+
+        def finish_z(c):
+            cols = slice(c * CHUNK, (c + 1) * CHUNK)
+            nc.vector.tensor_tensor(pairs[:, c, last // 2, :, last % 2], up[last][:, cols], emb_sb[last][:, cols], ADD)
+
+        def quantise_z(c):
+            grouped = keep.tile([P, CHUNK, PACK], BF16, name="z_grouped%d" % c, align_bytes=64)
+            src = pairs[:, c].rearrange("p u r e -> p r u e")
+            dst = grouped[:].rearrange("p r (u e) -> p r u e", e=2)
+            if c < CHUNKS - 1:
+                nc.scalar.copy(dst, src)
+            else:
+                nc.vector.tensor_copy(dst, src)
+            codes = keep.tile([P, CHUNK], U32, name="z_codes%d" % c, align_bytes=64)
+            scales = keep.tile([P, CHUNK], U8, name="z_scales%d" % c, align_bytes=64)
+            nc.vector.quantize_mx(
+                out=codes[:].bitcast(FP8X4), scales=scales[:], in_=grouped[:].rearrange("p r j -> p (r j)")
+            )
+            z_codes.append(codes)
+            z_scales.append(scales)
+
+        def second_product(m, c):
+            acc = bank((PACK + c if m == 0 else c), CHUNK, "y_acc%d_%d" % (m, c))
+            nc.tensor.matmul_mx(
+                out=acc[:],
+                lhsT=w2_codes[:, 2 * P * m : 2 * P * (m + 1)].bitcast(FP4X4),
+                lhsT_scale=w2_plane[:, P * m : P * (m + 1)],
+                rhs=z_codes[c][:].bitcast(FP8X4),
+                rhs_scale=z_scales[c][:],
+                start=True,
+                stop=True,
+            )
+            nc.scalar.activation(y[m][:, c * CHUNK : (c + 1) * CHUNK], acc[:], RELU)
+
+        for c in range(CHUNKS):
+            finish_z(c)
+        for c in range(CHUNKS):
+            quantise_z(c)
+            second_product(0, c)
+        for c in range(CHUNKS):
+            second_product(1, c)
+
+        def weighted(m, d, first, count):
+            part = keep.tile([P, count], F32, name="part%d_%d_%d" % (m, d, first))
+            nc.vector.tensor_tensor(
+                part[:], y[m][:].indirect(entries(pos_sb[d], first, count)), gate_sb[d][:, first : first + count], MULT
+            )
+            return part
+
+        def finish(m, first, count, a, b):
+            res = keep.tile([P, count], F32, name="res%d_%d" % (m, first))
+            nc.vector.tensor_tensor(res[:], a, b, ADD)
+            nc.sync.dma_start(out[P * m : P * (m + 1), first : first + count], res[:])
+
+        a0 = weighted(0, 0, 0, V)
+        b0 = weighted(0, 1, 0, V)
+        a1 = weighted(1, 0, 0, V)
+        finish(0, 0, V, a0[:], b0[:])
+        b1 = [weighted(1, 1, first, HALF) for first in range(0, V, HALF)]
+        for i, b in enumerate(b1):
+            finish(1, i * HALF, HALF, a1[:, i * HALF : (i + 1) * HALF], b[:])

@@ -25,6 +25,8 @@ HALF = 256
 CHUNK = 256
 CHUNKS = U // CHUNK
 SLOT_ORDER = (2, 0, 1, 3)
+PIECE = 128
+LEAD_PIECES = ((0, 128), (128, 128), (256, 256))
 
 
 def tile_picked_devox_relu_e_kernel(
@@ -58,8 +60,9 @@ def tile_picked_devox_relu_e_kernel(
         cell_sb = load_list(cell, "cell_sb")
         emb_rows = emb.rearrange("(p t) r -> p t r", t=PACK)
         emb_sb = {}
+
         for t in SLOT_ORDER:
-            emb_sb[t] = keep.tile([P, U], F32, name="emb%d" % t)
+            emb_sb[t] = keep.tile([P, U], F32, name="emb%d" % t, tag="emb%d" % t)
             nc.sync.dma_start(emb_sb[t][:], emb_rows[:, t, :])
         w2_codes = keep.tile([P, 2 * N], U8, name="w2_codes", align_bytes=64)
         nc.sync.dma_start(w2_codes[:].bitcast(I32), w2_words[0].bitcast(I32))
@@ -76,12 +79,12 @@ def tile_picked_devox_relu_e_kernel(
                 w2_plane[32 * q : 32 * q + 4, :].bitcast(I32), w2_scales[0, 4 * q : 4 * q + 4, :].bitcast(I32)
             )
 
-        def cleared_window(t, tag):
-            window = keep.tile([P, U], F32, name="up%d" % t, tag=tag)
+        def cleared_window(t):
+            window = keep.tile([P, U], F32, name="up%d" % t)
             nc.gpsimd.memset(window[:], 0.0)
             return window
 
-        up = {t: cleared_window(t, "up%d" % t) for t in SLOT_ORDER[:3]}
+        up = {t: cleared_window(t) for t in SLOT_ORDER}
 
         w1_grouped = keep.tile([P, PACK, P, PACK], BF16, name="w1_grouped", align_bytes=64)
         nc.scalar.activation(
@@ -93,27 +96,35 @@ def tile_picked_devox_relu_e_kernel(
             out=w1_codes[:].bitcast(FP8X4), scales=w1_plane[:], in_=w1_grouped[:].rearrange("p t m j -> p (t m j)")
         )
 
-        x_grouped = keep.tile([P, S, PACK], BF16, name="x_grouped", align_bytes=64)
+        x_pairs = keep.tile([P, S * PACK], BF16, name="x_pairs", align_bytes=64)
+        x_slots = x_pairs[:].rearrange("p (c u s e) -> p c u s e", u=2, s=PIECE, e=2)
+        x_words = x_pairs[:].bitcast(F32).rearrange("p (c u s) -> p c s u", u=2, s=PIECE)
         x_codes = keep.tile([P, S], U32, name="x_codes", align_bytes=64)
         x_scales = keep.tile([P, S], U8, name="x_scales", align_bytes=64)
         for j in range(PACK - 1):
-            nc.vector.tensor_copy(x_grouped[:, :, j], x_plane[j][:].indirect(offs_sb[:]))
+            nc.vector.tensor_copy(x_slots[:, :, j // 2, :, j % 2], x_plane[j][:].indirect(offs_sb[:]))
         for first in range(0, S, HALF):
             nc.vector.tensor_copy(
-                x_grouped[:, first : first + HALF, PACK - 1],
+                x_slots[:, first // PIECE : (first + HALF) // PIECE, 1, :, 1],
                 x_plane[PACK - 1][:].indirect(entries(offs_sb, first, HALF)),
             )
-        for first in range(0, S, HALF):
-            cols = slice(first, first + HALF)
-            nc.vector.quantize_mx(
-                out=x_codes[:, cols].bitcast(FP8X4),
-                scales=x_scales[:, cols],
-                in_=x_grouped[:, cols, :].rearrange("p s j -> p (s j)"),
+        x_grouped = []
+        for first, count in LEAD_PIECES:
+            grouped = keep.tile([P, count * PACK], BF16, name="x_grouped%d" % first, align_bytes=64)
+            nc.scalar.copy(
+                grouped[:].bitcast(F32).rearrange("p (c s u) -> p c s u", s=PIECE, u=2),
+                x_words[:, first // PIECE : (first + count) // PIECE],
             )
+            x_grouped.append(grouped)
+        for (first, count), grouped in zip(LEAD_PIECES, x_grouped):
+            cols = slice(first, first + count)
+            nc.vector.quantize_mx(out=x_codes[:, cols].bitcast(FP8X4), scales=x_scales[:, cols], in_=grouped[:])
 
-        pairs = keep.tile([P, CHUNKS, 2, CHUNK, 2], BF16, name="pairs", align_bytes=64)
+        z_pairs = keep.tile([P, U * PACK], BF16, name="z_pairs", align_bytes=64)
+        pairs = z_pairs[:].rearrange("p (c u r e) -> p c u r e", u=2, r=CHUNK, e=2)
+        z_words = z_pairs[:].bitcast(F32).rearrange("p (c u r) -> p c r u", u=2, r=CHUNK)
 
-        def first_product(t, first, count, bank_index):
+        def first_product(t, first, count, bank_index, tag):
             cols = slice(first, first + count)
             rows = slice(P * t, P * (t + 1))
             acc = bank(bank_index, count, "h_acc%d_%d" % (t, first))
@@ -126,7 +137,7 @@ def tile_picked_devox_relu_e_kernel(
                 start=True,
                 stop=True,
             )
-            h = keep.tile([P, count], F32, name="h%d_%d" % (t, first))
+            h = keep.tile([P, count], F32, name="h%d_%d" % (t, first), tag=tag)
             nc.scalar.activation(h[:], acc[:], RELU)
             return h
 
@@ -142,61 +153,51 @@ def tile_picked_devox_relu_e_kernel(
             )
 
         lead = SLOT_ORDER[0]
-        lead_halves = [first_product(lead, first, HALF, first // HALF) for first in range(0, S, HALF)]
-        h_rest = {t: first_product(t, 0, S, 2 + i) for i, t in enumerate(SLOT_ORDER[1:])}
-        for i, h in enumerate(lead_halves):
-            scatter(lead, h, i * HALF, HALF)
+        lead_parts = [first_product(lead, first, count, i, "h_lead%d" % i) for i, (first, count) in enumerate(LEAD_PIECES)]
+        h_rest = {t: first_product(t, 0, S, 3 + i, "h%d" % t) for i, t in enumerate(SLOT_ORDER[1:3])}
+        for (first, count), h in zip(LEAD_PIECES, lead_parts):
+            scatter(lead, h, first, count)
         add_emb_whole(lead)
         last = SLOT_ORDER[3]
-        up[last] = cleared_window(last, "up%d" % lead)
+        h_rest[last] = first_product(last, 0, S, 5, "emb%d" % lead)
         for t in SLOT_ORDER[1:3]:
             scatter(t, h_rest[t], 0, S)
             add_emb_whole(t)
         scatter(last, h_rest[last], 0, S)
 
         y = [keep.tile([P, U], F32, name="y%d" % m) for m in range(N // P)]
-        z_codes, z_scales = [], []
+        z_codes = keep.tile([P, U], U32, name="z_codes", align_bytes=64)
+        z_scales = keep.tile([P, U], U8, name="z_scales", align_bytes=64)
 
-        def finish_z(c):
-            cols = slice(c * CHUNK, (c + 1) * CHUNK)
-            nc.vector.tensor_tensor(pairs[:, c, last // 2, :, last % 2], up[last][:, cols], emb_sb[last][:, cols], ADD)
-
-        def quantise_z(c):
-            grouped = keep.tile([P, CHUNK, PACK], BF16, name="z_grouped%d" % c, align_bytes=64)
-            src = pairs[:, c].rearrange("p u r e -> p r u e")
-            dst = grouped[:].rearrange("p r (u e) -> p r u e", e=2)
-            if c < CHUNKS - 1:
-                nc.scalar.copy(dst, src)
-            else:
-                nc.vector.tensor_copy(dst, src)
-            codes = keep.tile([P, CHUNK], U32, name="z_codes%d" % c, align_bytes=64)
-            scales = keep.tile([P, CHUNK], U8, name="z_scales%d" % c, align_bytes=64)
-            nc.vector.quantize_mx(
-                out=codes[:].bitcast(FP8X4), scales=scales[:], in_=grouped[:].rearrange("p r j -> p (r j)")
-            )
-            z_codes.append(codes)
-            z_scales.append(scales)
-
-        def second_product(m, c):
-            acc = bank((PACK + c if m == 0 else c), CHUNK, "y_acc%d_%d" % (m, c))
+        def second_product(m, first, count, bank_index):
+            cols = slice(first, first + count)
+            acc = bank(bank_index, count, "y_acc%d_%d" % (m, first))
             nc.tensor.matmul_mx(
                 out=acc[:],
                 lhsT=w2_codes[:, 2 * P * m : 2 * P * (m + 1)].bitcast(FP4X4),
                 lhsT_scale=w2_plane[:, P * m : P * (m + 1)],
-                rhs=z_codes[c][:].bitcast(FP8X4),
-                rhs_scale=z_scales[c][:],
+                rhs=z_codes[:, cols].bitcast(FP8X4),
+                rhs_scale=z_scales[:, cols],
                 start=True,
                 stop=True,
             )
-            nc.scalar.activation(y[m][:, c * CHUNK : (c + 1) * CHUNK], acc[:], RELU)
+            nc.scalar.activation(y[m][:, cols], acc[:], RELU)
 
         for c in range(CHUNKS):
-            finish_z(c)
+            cols = slice(c * CHUNK, (c + 1) * CHUNK)
+            nc.vector.tensor_tensor(pairs[:, c, last // 2, :, last % 2], up[last][:, cols], emb_sb[last][:, cols], ADD)
+        z_grouped = []
         for c in range(CHUNKS):
-            quantise_z(c)
-            second_product(0, c)
+            grouped = keep.tile([P, CHUNK * PACK], BF16, name="z_grouped%d" % c, align_bytes=64)
+            nc.scalar.copy(grouped[:].bitcast(F32).rearrange("p (r u) -> p r u", u=2), z_words[:, c])
+            z_grouped.append(grouped)
         for c in range(CHUNKS):
-            second_product(1, c)
+            cols = slice(c * CHUNK, (c + 1) * CHUNK)
+            nc.vector.quantize_mx(out=z_codes[:, cols].bitcast(FP8X4), scales=z_scales[:, cols], in_=z_grouped[c][:])
+        for c in range(CHUNKS):
+            second_product(0, c * CHUNK, CHUNK, (6 + c) % 8)
+        for i in range(2):
+            second_product(1, i * 2 * CHUNK, 2 * CHUNK, i)
 
         def weighted(m, d, first, count):
             part = keep.tile([P, count], F32, name="part%d_%d_%d" % (m, d, first))

@@ -26,6 +26,8 @@ CHUNK = 256
 CHUNKS = U // CHUNK
 SLOT_ORDER = (2, 0, 1, 3)
 PIECE = 128
+Z_PIECES = ((0, 128), (128, 256), (384, 256), (640, 256), (896, 128))
+OUT_PIECES = ((0, 256), (256, 128), (384, 128))
 LEAD_PIECES = ((0, 128), (128, 128), (256, 256))
 
 
@@ -48,9 +50,9 @@ def tile_picked_devox_relu_e_kernel(
         def bank(index, width, name):
             return psum.tile([P, width], F32, name=name, tag="bank%d" % index)
 
-        offs_sb = load_list(offs, "offs_sb")
         w1_raw = keep.tile([P, PACK, H], F32, name="w1_raw")
         nc.sync.dma_start(w1_raw[:], w1.rearrange("(p j) c -> p j c", j=PACK))
+        offs_sb = load_list(offs, "offs_sb")
         x_rows = xT.rearrange("(p j) t -> p j t", j=PACK)
         x_plane = []
         for j in range(PACK):
@@ -69,7 +71,7 @@ def tile_picked_devox_relu_e_kernel(
         pos_sb = [load_list(pos1, "pos1_sb"), load_list(pos2, "pos2_sb")]
         gate_sb = []
         for d in range(2):
-            g = keep.tile([P, V], F32, name="gate%d" % d)
+            g = keep.tile([P, V], F32, name="gate%d" % d, tag="gate%d" % d)
             nc.sync.dma_start(g[:], gate[d])
             gate_sb.append(g)
         w2_plane = keep.tile([P, N], U8, name="w2_plane", align_bytes=64)
@@ -121,10 +123,10 @@ def tile_picked_devox_relu_e_kernel(
             nc.vector.quantize_mx(out=x_codes[:, cols].bitcast(FP8X4), scales=x_scales[:, cols], in_=grouped[:])
 
         z_pairs = keep.tile([P, U * PACK], BF16, name="z_pairs", align_bytes=64)
-        pairs = z_pairs[:].rearrange("p (c u r e) -> p c u r e", u=2, r=CHUNK, e=2)
-        z_words = z_pairs[:].bitcast(F32).rearrange("p (c u r) -> p c r u", u=2, r=CHUNK)
+        pairs = z_pairs[:].rearrange("p (c u r e) -> p c u r e", u=2, r=PIECE, e=2)
+        z_words = z_pairs[:].bitcast(F32).rearrange("p (c u r) -> p c r u", u=2, r=PIECE)
 
-        def first_product(t, first, count, bank_index, tag):
+        def first_product(t, first, count, bank_index, h):
             cols = slice(first, first + count)
             rows = slice(P * t, P * (t + 1))
             acc = bank(bank_index, count, "h_acc%d_%d" % (t, first))
@@ -137,39 +139,43 @@ def tile_picked_devox_relu_e_kernel(
                 start=True,
                 stop=True,
             )
-            h = keep.tile([P, count], F32, name="h%d_%d" % (t, first), tag=tag)
-            nc.scalar.activation(h[:], acc[:], RELU)
-            return h
+            nc.scalar.activation(h, acc[:], RELU)
 
         def scatter(t, h, first, count):
-            nc.vector.tensor_copy(up[t][:].indirect(entries(cell_sb, first, count)), h[:])
+            nc.vector.tensor_copy(up[t][:].indirect(entries(cell_sb, first, count)), h)
 
         def add_emb_whole(t):
             nc.gpsimd.tensor_tensor(
                 pairs[:, :, t // 2, :, t % 2],
-                up[t][:].rearrange("p (c r) -> p c r", r=CHUNK),
-                emb_sb[t][:].rearrange("p (c r) -> p c r", r=CHUNK),
+                up[t][:].rearrange("p (c r) -> p c r", r=PIECE),
+                emb_sb[t][:].rearrange("p (c r) -> p c r", r=PIECE),
                 ADD,
             )
 
-        lead = SLOT_ORDER[0]
-        lead_parts = [first_product(lead, first, count, i, "h_lead%d" % i) for i, (first, count) in enumerate(LEAD_PIECES)]
-        h_rest = {t: first_product(t, 0, S, 3 + i, "h%d" % t) for i, t in enumerate(SLOT_ORDER[1:3])}
-        for (first, count), h in zip(LEAD_PIECES, lead_parts):
-            scatter(lead, h, first, count)
-        add_emb_whole(lead)
-        last = SLOT_ORDER[3]
-        h_rest[last] = first_product(last, 0, S, 5, "emb%d" % lead)
-        for t in SLOT_ORDER[1:3]:
-            scatter(t, h_rest[t], 0, S)
+        early, third, last = SLOT_ORDER[:2], SLOT_ORDER[2], SLOT_ORDER[3]
+        h = {t: keep.tile([P, S], F32, name="h%d" % t) for t in SLOT_ORDER[:3]}
+        for i, t in enumerate(early):
+            first_product(t, 0, PIECE, i, h[t][:, :PIECE])
+        for i, t in enumerate(early):
+            for n, (first, count) in enumerate(LEAD_PIECES[1:]):
+                first_product(t, first, count, 2 + 2 * i + n, h[t][:, first : first + count])
+        first_product(third, 0, S, 6, h[third][:])
+        for t in early:
+            scatter(t, h[t][:, :PIECE], 0, PIECE)
+        for t in early:
+            scatter(t, h[t][:, PIECE:], PIECE, S - PIECE)
             add_emb_whole(t)
-        scatter(last, h_rest[last], 0, S)
+        h[last] = keep.tile([P, S], F32, name="h%d" % last, tag="emb%d" % early[0])
+        first_product(last, 0, S, 7, h[last][:])
+        scatter(third, h[third][:], 0, S)
+        add_emb_whole(third)
+        scatter(last, h[last][:], 0, S)
 
         y = [keep.tile([P, U], F32, name="y%d" % m) for m in range(N // P)]
         z_codes = keep.tile([P, U], U32, name="z_codes", align_bytes=64)
         z_scales = keep.tile([P, U], U8, name="z_scales", align_bytes=64)
 
-        def second_product(m, first, count, bank_index):
+        def second_product(m, first, count, bank_index, on_vector):
             cols = slice(first, first + count)
             acc = bank(bank_index, count, "y_acc%d_%d" % (m, first))
             nc.tensor.matmul_mx(
@@ -181,23 +187,33 @@ def tile_picked_devox_relu_e_kernel(
                 start=True,
                 stop=True,
             )
-            nc.scalar.activation(y[m][:, cols], acc[:], RELU)
+            if on_vector:
+                nc.vector.tensor_scalar_max(y[m][:, cols], acc[:], 0.0)
+            else:
+                nc.scalar.activation(y[m][:, cols], acc[:], RELU)
 
-        for c in range(CHUNKS):
-            cols = slice(c * CHUNK, (c + 1) * CHUNK)
-            nc.vector.tensor_tensor(pairs[:, c, last // 2, :, last % 2], up[last][:, cols], emb_sb[last][:, cols], ADD)
+        for first, count in Z_PIECES:
+            nc.vector.tensor_tensor(
+                pairs[:, first // PIECE : (first + count) // PIECE, last // 2, :, last % 2],
+                up[last][:, first : first + count].rearrange("p (c r) -> p c r", r=PIECE),
+                emb_sb[last][:, first : first + count].rearrange("p (c r) -> p c r", r=PIECE),
+                ADD,
+            )
         z_grouped = []
-        for c in range(CHUNKS):
-            grouped = keep.tile([P, CHUNK * PACK], BF16, name="z_grouped%d" % c, align_bytes=64)
-            nc.scalar.copy(grouped[:].bitcast(F32).rearrange("p (r u) -> p r u", u=2), z_words[:, c])
+        for first, count in Z_PIECES:
+            grouped = keep.tile([P, count * PACK], BF16, name="z_grouped%d" % first, align_bytes=64)
+            nc.scalar.copy(
+                grouped[:].bitcast(F32).rearrange("p (c r u) -> p c r u", r=PIECE, u=2),
+                z_words[:, first // PIECE : (first + count) // PIECE],
+            )
             z_grouped.append(grouped)
-        for c in range(CHUNKS):
-            cols = slice(c * CHUNK, (c + 1) * CHUNK)
-            nc.vector.quantize_mx(out=z_codes[:, cols].bitcast(FP8X4), scales=z_scales[:, cols], in_=z_grouped[c][:])
-        for c in range(CHUNKS):
-            second_product(0, c * CHUNK, CHUNK, (6 + c) % 8)
+        for (first, count), grouped in zip(Z_PIECES, z_grouped):
+            cols = slice(first, first + count)
+            nc.vector.quantize_mx(out=z_codes[:, cols].bitcast(FP8X4), scales=z_scales[:, cols], in_=grouped[:])
+        for i, (first, count) in enumerate(Z_PIECES):
+            second_product(0, first, count, i, i == len(Z_PIECES) - 2)
         for i in range(2):
-            second_product(1, i * 2 * CHUNK, 2 * CHUNK, i)
+            second_product(1, i * U // 2, U // 2, len(Z_PIECES) - 2 + i, False)
 
         def weighted(m, d, first, count):
             part = keep.tile([P, count], F32, name="part%d_%d_%d" % (m, d, first))
@@ -206,15 +222,17 @@ def tile_picked_devox_relu_e_kernel(
             )
             return part
 
-        def finish(m, first, count, a, b):
-            res = keep.tile([P, count], F32, name="res%d_%d" % (m, first))
+        def finish(m, first, count, a, b, tag):
+            res = keep.tile([P, count], F32, name="res%d_%d" % (m, first), tag=tag)
             nc.vector.tensor_tensor(res[:], a, b, ADD)
             nc.sync.dma_start(out[P * m : P * (m + 1), first : first + count], res[:])
 
         a0 = weighted(0, 0, 0, V)
         b0 = weighted(0, 1, 0, V)
         a1 = weighted(1, 0, 0, V)
-        finish(0, 0, V, a0[:], b0[:])
-        b1 = [weighted(1, 1, first, HALF) for first in range(0, V, HALF)]
-        for i, b in enumerate(b1):
-            finish(1, i * HALF, HALF, a1[:, i * HALF : (i + 1) * HALF], b[:])
+        pending = (0, 0, V, a0[:], b0[:], "gate0")
+        for first, count in OUT_PIECES:
+            b1 = weighted(1, 1, first, count)
+            finish(*pending)
+            pending = (1, first, count, a1[:, first : first + count], b1[:], "res%d" % first)
+        finish(*pending)

@@ -1,6 +1,7 @@
 from contextlib import ExitStack
 
 import concourse.mybir as mybir
+from concourse.masks import make_identity
 
 K, T, S, V, H, N, U = 512, 2048, 512, 512, 512, 256, 1024
 FLOPS = 2 * K * H * S + 2 * H * N * U
@@ -50,8 +51,14 @@ def tile_picked_devox_relu_e_kernel(
         def bank(index, width, name):
             return psum.tile([P, width], F32, name=name, tag="bank%d" % index)
 
-        w1_raw = keep.tile([P, PACK, H], F32, name="w1_raw")
-        nc.sync.dma_start(w1_raw[:], w1.rearrange("(p j) c -> p j c", j=PACK))
+        w1_rows = w1.rearrange("(p j) c -> p j c", j=PACK)
+
+        def load_w1_half(half):
+            raw = keep.tile([P, 2, H], F32, name="w1_raw%d" % half)
+            nc.sync.dma_start(raw[:], w1_rows[:, 2 * half : 2 * half + 2, :])
+            return raw
+
+        w1_raw = [load_w1_half(0)]
         offs_sb = load_list(offs, "offs_sb")
         x_rows = xT.rearrange("(p j) t -> p j t", j=PACK)
         x_plane = []
@@ -59,6 +66,7 @@ def tile_picked_devox_relu_e_kernel(
             plane = keep.tile([P, T], F32, name="x_plane%d" % j)
             nc.sync.dma_start(plane[:], x_rows[:, j, :])
             x_plane.append(plane)
+        w1_raw.append(load_w1_half(1))
         cell_sb = load_list(cell, "cell_sb")
         emb_rows = emb.rearrange("(p t) r -> p t r", t=PACK)
         emb_sb = {}
@@ -88,21 +96,42 @@ def tile_picked_devox_relu_e_kernel(
 
         up = {t: cleared_window(t) for t in SLOT_ORDER}
 
-        w1_grouped = keep.tile([P, PACK, P, PACK], BF16, name="w1_grouped", align_bytes=64)
-        nc.scalar.activation(
-            w1_grouped[:].rearrange("p t m j -> p m t j"), w1_raw[:].rearrange("p j (m t) -> p m t j", t=PACK), COPY
-        )
+        ident = keep.tile([P, P], F32, name="ident")
+        make_identity(nc, ident[:])
+
         w1_codes = keep.tile([P, H], U32, name="w1_codes", align_bytes=64)
         w1_plane = keep.tile([P, H], U8, name="w1_plane", align_bytes=64)
-        nc.vector.quantize_mx(
-            out=w1_codes[:].bitcast(FP8X4), scales=w1_plane[:], in_=w1_grouped[:].rearrange("p t m j -> p (t m j)")
-        )
+
+        early, third, last = SLOT_ORDER[:2], SLOT_ORDER[2], SLOT_ORDER[3]
+        w1_one = {
+            t: keep.tile([P, P * PACK], BF16, name="w1_one%d" % t, tag="held%d" % t, align_bytes=64) for t in early
+        }
+        w1_odd = keep.tile([P, 2 * P * PACK], BF16, name="w1_odd", align_bytes=64)
+
+        def one_views(half, t):
+            return (
+                w1_one[t][:].rearrange("p (m h j) -> p h m j", h=2, j=2)[:, half],
+                w1_raw[half][:].rearrange("p j (m t) -> p t m j", t=PACK)[:, t],
+            )
+
+        def group_odd(half):
+            nc.scalar.activation(
+                w1_odd[:].rearrange("p (u m h j) -> p h m u j", u=2, h=2, j=2)[:, half],
+                w1_raw[half][:].rearrange("p j (m u e) -> p e m u j", u=2, e=2)[:, 1],
+                COPY,
+            )
+
+        def quantise_w1(t, grouped):
+            rows = slice(P * t, P * (t + 1))
+            nc.vector.quantize_mx(out=w1_codes[:, rows].bitcast(FP8X4), scales=w1_plane[:, rows], in_=grouped)
+
+        for t in early:
+            nc.scalar.activation(*one_views(0, t), COPY)
+        group_odd(0)
 
         x_pairs = keep.tile([P, S * PACK], BF16, name="x_pairs", align_bytes=64)
         x_slots = x_pairs[:].rearrange("p (c u s e) -> p c u s e", u=2, s=PIECE, e=2)
         x_words = x_pairs[:].bitcast(F32).rearrange("p (c u s) -> p c s u", u=2, s=PIECE)
-        x_codes = keep.tile([P, S], U32, name="x_codes", align_bytes=64)
-        x_scales = keep.tile([P, S], U8, name="x_scales", align_bytes=64)
         for j in range(PACK - 1):
             nc.vector.tensor_copy(x_slots[:, :, j // 2, :, j % 2], x_plane[j][:].indirect(offs_sb[:]))
         for first in range(0, S, HALF):
@@ -118,27 +147,45 @@ def tile_picked_devox_relu_e_kernel(
                 x_words[:, first // PIECE : (first + count) // PIECE],
             )
             x_grouped.append(grouped)
-        for (first, count), grouped in zip(LEAD_PIECES, x_grouped):
-            cols = slice(first, first + count)
-            nc.vector.quantize_mx(out=x_codes[:, cols].bitcast(FP8X4), scales=x_scales[:, cols], in_=grouped[:])
+        x_mx = []
+
+        def quantise_x(i, tag):
+            count = LEAD_PIECES[i][1]
+            codes = keep.tile([P, count], U32, name="x_codes%d" % i, tag=tag, align_bytes=64)
+            scales = keep.tile([P, count], U8, name="x_scales%d" % i, align_bytes=64)
+            nc.vector.quantize_mx(out=codes[:].bitcast(FP8X4), scales=scales[:], in_=x_grouped[i][:])
+            x_mx.append((codes, scales))
+
+        quantise_x(0, "x_codes0")
+        for t in early:
+            nc.vector.tensor_copy(*one_views(1, t))
+        for t in early:
+            quantise_w1(t, w1_one[t][:])
+        for i, t in enumerate(early):
+            quantise_x(1 + i, "held%d" % t)
+        group_odd(1)
+        for u in range(2):
+            quantise_w1(2 * u + 1, w1_odd[:, u * P * PACK : (u + 1) * P * PACK])
 
         z_pairs = keep.tile([P, U * PACK], BF16, name="z_pairs", align_bytes=64)
         pairs = z_pairs[:].rearrange("p (c u r e) -> p c u r e", u=2, r=PIECE, e=2)
         z_words = z_pairs[:].bitcast(F32).rearrange("p (c u r) -> p c r u", u=2, r=PIECE)
 
-        def first_product(t, first, count, bank_index, h):
-            cols = slice(first, first + count)
+        def first_product(t, pieces, bank_index, h):
             rows = slice(P * t, P * (t + 1))
-            acc = bank(bank_index, count, "h_acc%d_%d" % (t, first))
-            nc.tensor.matmul_mx(
-                out=acc[:],
-                lhsT=w1_codes[:, rows].bitcast(FP8X4),
-                lhsT_scale=w1_plane[:, rows],
-                rhs=x_codes[:, cols].bitcast(FP8X4),
-                rhs_scale=x_scales[:, cols],
-                start=True,
-                stop=True,
-            )
+            base = LEAD_PIECES[pieces[0]][0]
+            acc = bank(bank_index, sum(LEAD_PIECES[i][1] for i in pieces), "h_acc%d_%d" % (t, base))
+            for i in pieces:
+                first, count = LEAD_PIECES[i]
+                nc.tensor.matmul_mx(
+                    out=acc[:, first - base : first - base + count],
+                    lhsT=w1_codes[:, rows].bitcast(FP8X4),
+                    lhsT_scale=w1_plane[:, rows],
+                    rhs=x_mx[i][0][:].bitcast(FP8X4),
+                    rhs_scale=x_mx[i][1][:],
+                    start=True,
+                    stop=True,
+                )
             nc.scalar.activation(h, acc[:], RELU)
 
         def scatter(t, h, first, count):
@@ -152,21 +199,19 @@ def tile_picked_devox_relu_e_kernel(
                 ADD,
             )
 
-        early, third, last = SLOT_ORDER[:2], SLOT_ORDER[2], SLOT_ORDER[3]
         h = {t: keep.tile([P, S], F32, name="h%d" % t) for t in SLOT_ORDER[:3]}
         for i, t in enumerate(early):
-            first_product(t, 0, PIECE, i, h[t][:, :PIECE])
+            first_product(t, (0,), i, h[t][:, :PIECE])
         for i, t in enumerate(early):
-            for n, (first, count) in enumerate(LEAD_PIECES[1:]):
-                first_product(t, first, count, 2 + 2 * i + n, h[t][:, first : first + count])
-        first_product(third, 0, S, 6, h[third][:])
+            first_product(t, (1, 2), 2 + i, h[t][:, PIECE:])
+        first_product(third, (0, 1, 2), 4, h[third][:])
         for t in early:
             scatter(t, h[t][:, :PIECE], 0, PIECE)
         for t in early:
             scatter(t, h[t][:, PIECE:], PIECE, S - PIECE)
             add_emb_whole(t)
         h[last] = keep.tile([P, S], F32, name="h%d" % last, tag="emb%d" % early[0])
-        first_product(last, 0, S, 7, h[last][:])
+        first_product(last, (0, 1, 2), 5, h[last][:])
         scatter(third, h[third][:], 0, S)
         add_emb_whole(third)
         scatter(last, h[last][:], 0, S)
@@ -211,9 +256,9 @@ def tile_picked_devox_relu_e_kernel(
             cols = slice(first, first + count)
             nc.vector.quantize_mx(out=z_codes[:, cols].bitcast(FP8X4), scales=z_scales[:, cols], in_=grouped[:])
         for i, (first, count) in enumerate(Z_PIECES):
-            second_product(0, first, count, i, i == len(Z_PIECES) - 2)
-        for i in range(2):
-            second_product(1, i * U // 2, U // 2, len(Z_PIECES) - 2 + i, False)
+            second_product(0, first, count, i, i >= len(Z_PIECES) - 2)
+        for i, (first, count) in enumerate(Z_PIECES):
+            second_product(1, first, count, (len(Z_PIECES) + i) % 8, False)
 
         def weighted(m, d, first, count):
             part = keep.tile([P, count], F32, name="part%d_%d_%d" % (m, d, first))
@@ -227,12 +272,32 @@ def tile_picked_devox_relu_e_kernel(
             nc.vector.tensor_tensor(res[:], a, b, ADD)
             nc.sync.dma_start(out[P * m : P * (m + 1), first : first + count], res[:])
 
-        a0 = weighted(0, 0, 0, V)
-        b0 = weighted(0, 1, 0, V)
+        for i, first in enumerate(range(0, V, HALF)):
+            turned = bank(2 + i, HALF, "turned%d" % i)
+            parts = [weighted(0, d, first, HALF) for d in range(2)]
+            order = [(part, n) for part in parts for n in range(2)]
+            for step, (part, n) in enumerate(order):
+                nc.tensor.matmul(
+                    turned[:, P * n : P * (n + 1)],
+                    lhsT=part[:, P * n : P * (n + 1)],
+                    rhs=ident[:],
+                    is_transpose=True,
+                    start=step == 0,
+                    stop=step == len(order) - 1,
+                )
+            sums = keep.tile([P, HALF], F32, name="sums%d" % i)
+            nc.scalar.copy(sums[:], turned[:])
+            back = bank(4 + i, HALF, "back%d" % i)
+            for n in range(2):
+                nc.tensor.transpose(back[:, P * n : P * (n + 1)], sums[:, P * n : P * (n + 1)], ident[:])
+            res = keep.tile([P, HALF], F32, name="res0_%d" % i)
+            nc.scalar.copy(res[:], back[:])
+            nc.scalar.dma_start(out[0:P, first : first + HALF], res[:])
         a1 = weighted(1, 0, 0, V)
-        pending = (0, 0, V, a0[:], b0[:], "gate0")
+        pending = None
         for first, count in OUT_PIECES:
             b1 = weighted(1, 1, first, count)
-            finish(*pending)
+            if pending is not None:
+                finish(*pending)
             pending = (1, first, count, a1[:, first : first + count], b1[:], "res%d" % first)
         finish(*pending)

@@ -191,12 +191,13 @@ def tile_picked_devox_relu_e_kernel(
         def scatter(t, h, first, count):
             nc.vector.tensor_copy(up[t][:].indirect(entries(cell_sb, first, count)), h)
 
-        def add_emb_whole(t):
-            nc.gpsimd.tensor_tensor(
-                pairs[:, :, t // 2, :, t % 2],
-                up[t][:].rearrange("p (c r) -> p c r", r=PIECE),
-                emb_sb[t][:].rearrange("p (c r) -> p c r", r=PIECE),
-                ADD,
+        def add_emb(t, first, count):
+            cols = slice(first, first + count)
+            plane = keep.tile([P, count], BF16, name="z%d_%d" % (t, first), tag="z%d_%d" % (t, first))
+            nc.gpsimd.tensor_tensor(plane[:], up[t][:, cols], emb_sb[t][:, cols], ADD)
+            nc.scalar.copy(
+                pairs[:, first // PIECE : (first + count) // PIECE, t // 2, :, t % 2],
+                plane[:].rearrange("p (c r) -> p c r", r=PIECE),
             )
 
         h = {t: keep.tile([P, S], F32, name="h%d" % t) for t in SLOT_ORDER[:3]}
@@ -209,11 +210,18 @@ def tile_picked_devox_relu_e_kernel(
             scatter(t, h[t][:, :PIECE], 0, PIECE)
         for t in early:
             scatter(t, h[t][:, PIECE:], PIECE, S - PIECE)
-            add_emb_whole(t)
+        nc.gpsimd.tensor_tensor(
+            pairs[:, :, early[0] // 2, :, early[0] % 2],
+            up[early[0]][:].rearrange("p (c r) -> p c r", r=PIECE),
+            emb_sb[early[0]][:].rearrange("p (c r) -> p c r", r=PIECE),
+            ADD,
+        )
         h[last] = keep.tile([P, S], F32, name="h%d" % last, tag="emb%d" % early[0])
-        first_product(last, (0, 1, 2), 5, h[last][:])
+        first_product(last, ((0, 1, 2)), 5, h[last][:])
+        add_emb(early[1], 0, U)
         scatter(third, h[third][:], 0, S)
-        add_emb_whole(third)
+        for first in range(0, U, U // 2):
+            add_emb(third, first, U // 2)
         scatter(last, h[last][:], 0, S)
 
         y = [keep.tile([P, U], F32, name="y%d" % m) for m in range(N // P)]

from contextlib import ExitStack

import concourse.mybir as mybir
from concourse.masks import make_identity

K, T, S, V, H, N, U = 512, 2048, 512, 512, 512, 256, 1024
FLOPS = 2 * K * H * S + 2 * H * N * U

F32 = mybir.dt.float32
BF16 = mybir.dt.bfloat16
I32 = mybir.dt.int32
U32 = mybir.dt.uint32
U16 = mybir.dt.uint16
U8 = mybir.dt.uint8
FP8X4 = mybir.dt.float8_e4m3fn_x4
FP4X4 = mybir.dt.float4_e2m1fn_x4
ADD = mybir.AluOpType.add
MULT = mybir.AluOpType.mult
RELU = mybir.ActivationFunctionType.Relu
COPY = mybir.ActivationFunctionType.Copy

P = 128
PACK = 4
LIST_ROWS = 16
HALF = 256
CHUNK = 256
CHUNKS = U // CHUNK
SLOT_ORDER = (2, 0, 1, 3)
PIECE = 128
Z_PIECES = ((0, 128), (128, 256), (384, 256), (640, 256), (896, 128))
OUT_PIECES = ((0, 256), (256, 128), (384, 128))
LEAD_PIECES = ((0, 128), (128, 128), (256, 256))


def tile_picked_devox_relu_e_kernel(
    tc, xT, w1, w2_words, w2_scales, gate, emb, offs, cell, pos1, pos2, out
):
    nc = tc.nc
    with ExitStack() as ctx:
        keep = ctx.enter_context(tc.tile_pool(name="keep", bufs=1))
        psum = ctx.enter_context(tc.psum_pool(name="psum", bufs=1))

        def load_list(src, name):
            tile = keep.tile([P, src.shape[1]], U16, name=name)
            nc.sync.dma_start(tile[:], src)
            return tile

        def entries(lst, first, count):
            return lst[:, first // LIST_ROWS : (first + count) // LIST_ROWS]

        def bank(index, width, name):
            return psum.tile([P, width], F32, name=name, tag="bank%d" % index)

        w1_rows = w1.rearrange("(p j) c -> p j c", j=PACK)

        def load_w1_half(half):
            raw = keep.tile([P, 2, H], F32, name="w1_raw%d" % half)
            nc.sync.dma_start(raw[:], w1_rows[:, 2 * half : 2 * half + 2, :])
            return raw

        w1_raw = [load_w1_half(0)]
        offs_sb = load_list(offs, "offs_sb")
        x_rows = xT.rearrange("(p j) t -> p j t", j=PACK)
        x_plane = []
        for j in range(PACK):
            plane = keep.tile([P, T], F32, name="x_plane%d" % j)
            nc.sync.dma_start(plane[:], x_rows[:, j, :])
            x_plane.append(plane)
        w1_raw.append(load_w1_half(1))
        cell_sb = load_list(cell, "cell_sb")
        emb_rows = emb.rearrange("(p t) r -> p t r", t=PACK)
        emb_sb = {}

        for t in SLOT_ORDER:
            emb_sb[t] = keep.tile([P, U], F32, name="emb%d" % t, tag="emb%d" % t)
            nc.sync.dma_start(emb_sb[t][:], emb_rows[:, t, :])
        w2_codes = keep.tile([P, 2 * N], U8, name="w2_codes", align_bytes=64)
        nc.sync.dma_start(w2_codes[:].bitcast(I32), w2_words[0].bitcast(I32))
        pos_sb = [load_list(pos1, "pos1_sb"), load_list(pos2, "pos2_sb")]
        gate_sb = []
        for d in range(2):
            g = keep.tile([P, V], F32, name="gate%d" % d, tag="gate%d" % d)
            nc.sync.dma_start(g[:], gate[d])
            gate_sb.append(g)
        w2_plane = keep.tile([P, N], U8, name="w2_plane", align_bytes=64)
        nc.gpsimd.memset(w2_plane[:], 0)
        for q in range(4):
            nc.sync.dma_start(
                w2_plane[32 * q : 32 * q + 4, :].bitcast(I32), w2_scales[0, 4 * q : 4 * q + 4, :].bitcast(I32)
            )

        def cleared_window(t):
            window = keep.tile([P, U], F32, name="up%d" % t)
            nc.gpsimd.memset(window[:], 0.0)
            return window

        up = {t: cleared_window(t) for t in SLOT_ORDER}

        ident = keep.tile([P, P], F32, name="ident")
        make_identity(nc, ident[:])

        w1_codes = keep.tile([P, H], U32, name="w1_codes", align_bytes=64)
        w1_plane = keep.tile([P, H], U8, name="w1_plane", align_bytes=64)

        early, third, last = SLOT_ORDER[:2], SLOT_ORDER[2], SLOT_ORDER[3]
        w1_one = {
            t: keep.tile([P, P * PACK], BF16, name="w1_one%d" % t, tag="held%d" % t, align_bytes=64) for t in early
        }
        w1_odd = keep.tile([P, 2 * P * PACK], BF16, name="w1_odd", align_bytes=64)

        def one_views(half, t):
            return (
                w1_one[t][:].rearrange("p (m h j) -> p h m j", h=2, j=2)[:, half],
                w1_raw[half][:].rearrange("p j (m t) -> p t m j", t=PACK)[:, t],
            )

        def group_odd(half):
            nc.scalar.activation(
                w1_odd[:].rearrange("p (u m h j) -> p h m u j", u=2, h=2, j=2)[:, half],
                w1_raw[half][:].rearrange("p j (m u e) -> p e m u j", u=2, e=2)[:, 1],
                COPY,
            )

        def quantise_w1(t, grouped):
            rows = slice(P * t, P * (t + 1))
            nc.vector.quantize_mx(out=w1_codes[:, rows].bitcast(FP8X4), scales=w1_plane[:, rows], in_=grouped)

        for t in early:
            nc.scalar.activation(*one_views(0, t), COPY)
        group_odd(0)

        x_pairs = keep.tile([P, S * PACK], BF16, name="x_pairs", align_bytes=64)
        x_slots = x_pairs[:].rearrange("p (c u s e) -> p c u s e", u=2, s=PIECE, e=2)
        x_words = x_pairs[:].bitcast(F32).rearrange("p (c u s) -> p c s u", u=2, s=PIECE)
        for j in range(PACK - 1):
            nc.vector.tensor_copy(x_slots[:, :, j // 2, :, j % 2], x_plane[j][:].indirect(offs_sb[:]))
        for first in range(0, S, HALF):
            nc.vector.tensor_copy(
                x_slots[:, first // PIECE : (first + HALF) // PIECE, 1, :, 1],
                x_plane[PACK - 1][:].indirect(entries(offs_sb, first, HALF)),
            )
        x_grouped = []
        for first, count in LEAD_PIECES:
            grouped = keep.tile([P, count * PACK], BF16, name="x_grouped%d" % first, align_bytes=64)
            nc.scalar.copy(
                grouped[:].bitcast(F32).rearrange("p (c s u) -> p c s u", s=PIECE, u=2),
                x_words[:, first // PIECE : (first + count) // PIECE],
            )
            x_grouped.append(grouped)
        x_mx = []

        def quantise_x(i, tag):
            count = LEAD_PIECES[i][1]
            codes = keep.tile([P, count], U32, name="x_codes%d" % i, tag=tag, align_bytes=64)
            scales = keep.tile([P, count], U8, name="x_scales%d" % i, align_bytes=64)
            nc.vector.quantize_mx(out=codes[:].bitcast(FP8X4), scales=scales[:], in_=x_grouped[i][:])
            x_mx.append((codes, scales))

        quantise_x(0, "x_codes0")
        for t in early:
            nc.vector.tensor_copy(*one_views(1, t))
        for t in early:
            quantise_w1(t, w1_one[t][:])
        for i, t in enumerate(early):
            quantise_x(1 + i, "held%d" % t)
        group_odd(1)
        for u in range(2):
            quantise_w1(2 * u + 1, w1_odd[:, u * P * PACK : (u + 1) * P * PACK])

        z_pairs = keep.tile([P, U * PACK], BF16, name="z_pairs", align_bytes=64)
        pairs = z_pairs[:].rearrange("p (c u r e) -> p c u r e", u=2, r=PIECE, e=2)
        z_words = z_pairs[:].bitcast(F32).rearrange("p (c u r) -> p c r u", u=2, r=PIECE)

        def first_product(t, pieces, bank_index, h):
            rows = slice(P * t, P * (t + 1))
            base = LEAD_PIECES[pieces[0]][0]
            acc = bank(bank_index, sum(LEAD_PIECES[i][1] for i in pieces), "h_acc%d_%d" % (t, base))
            for i in pieces:
                first, count = LEAD_PIECES[i]
                nc.tensor.matmul_mx(
                    out=acc[:, first - base : first - base + count],
                    lhsT=w1_codes[:, rows].bitcast(FP8X4),
                    lhsT_scale=w1_plane[:, rows],
                    rhs=x_mx[i][0][:].bitcast(FP8X4),
                    rhs_scale=x_mx[i][1][:],
                    start=True,
                    stop=True,
                )
            nc.scalar.activation(h, acc[:], RELU)

        def scatter(t, h, first, count):
            nc.vector.tensor_copy(up[t][:].indirect(entries(cell_sb, first, count)), h)

        def add_emb(t, first, count):
            cols = slice(first, first + count)
            plane = keep.tile([P, count], BF16, name="z%d_%d" % (t, first), tag="z%d_%d" % (t, first))
            nc.gpsimd.tensor_tensor(plane[:], up[t][:, cols], emb_sb[t][:, cols], ADD)
            nc.scalar.copy(
                pairs[:, first // PIECE : (first + count) // PIECE, t // 2, :, t % 2],
                plane[:].rearrange("p (c r) -> p c r", r=PIECE),
            )

        h = {t: keep.tile([P, S], F32, name="h%d" % t) for t in SLOT_ORDER[:3]}
        for i, t in enumerate(early):
            first_product(t, (0,), i, h[t][:, :PIECE])
        for i, t in enumerate(early):
            first_product(t, (1, 2), 2 + i, h[t][:, PIECE:])
        first_product(third, (0, 1, 2), 4, h[third][:])
        for t in early:
            scatter(t, h[t][:, :PIECE], 0, PIECE)
        for t in early:
            scatter(t, h[t][:, PIECE:], PIECE, S - PIECE)
        nc.gpsimd.tensor_tensor(
            pairs[:, :, early[0] // 2, :, early[0] % 2],
            up[early[0]][:].rearrange("p (c r) -> p c r", r=PIECE),
            emb_sb[early[0]][:].rearrange("p (c r) -> p c r", r=PIECE),
            ADD,
        )
        h[last] = keep.tile([P, S], F32, name="h%d" % last, tag="emb%d" % early[0])
        first_product(last, ((0, 1, 2)), 5, h[last][:])
        add_emb(early[1], 0, U)
        scatter(third, h[third][:], 0, S)
        for first in range(0, U, U // 2):
            add_emb(third, first, U // 2)
        scatter(last, h[last][:], 0, S)

        y = [keep.tile([P, U], F32, name="y%d" % m) for m in range(N // P)]
        z_codes = keep.tile([P, U], U32, name="z_codes", align_bytes=64)
        z_scales = keep.tile([P, U], U8, name="z_scales", align_bytes=64)

        def second_product(m, first, count, bank_index, on_vector):
            cols = slice(first, first + count)
            acc = bank(bank_index, count, "y_acc%d_%d" % (m, first))
            nc.tensor.matmul_mx(
                out=acc[:],
                lhsT=w2_codes[:, 2 * P * m : 2 * P * (m + 1)].bitcast(FP4X4),
                lhsT_scale=w2_plane[:, P * m : P * (m + 1)],
                rhs=z_codes[:, cols].bitcast(FP8X4),
                rhs_scale=z_scales[:, cols],
                start=True,
                stop=True,
            )
            if on_vector:
                nc.vector.tensor_scalar_max(y[m][:, cols], acc[:], 0.0)
            else:
                nc.scalar.activation(y[m][:, cols], acc[:], RELU)

        for first, count in Z_PIECES:
            nc.vector.tensor_tensor(
                pairs[:, first // PIECE : (first + count) // PIECE, last // 2, :, last % 2],
                up[last][:, first : first + count].rearrange("p (c r) -> p c r", r=PIECE),
                emb_sb[last][:, first : first + count].rearrange("p (c r) -> p c r", r=PIECE),
                ADD,
            )
        z_grouped = []
        for first, count in Z_PIECES:
            grouped = keep.tile([P, count * PACK], BF16, name="z_grouped%d" % first, align_bytes=64)
            nc.scalar.copy(
                grouped[:].bitcast(F32).rearrange("p (c r u) -> p c r u", r=PIECE, u=2),
                z_words[:, first // PIECE : (first + count) // PIECE],
            )
            z_grouped.append(grouped)
        for (first, count), grouped in zip(Z_PIECES, z_grouped):
            cols = slice(first, first + count)
            nc.vector.quantize_mx(out=z_codes[:, cols].bitcast(FP8X4), scales=z_scales[:, cols], in_=grouped[:])
        for i, (first, count) in enumerate(Z_PIECES):
            second_product(0, first, count, i, i >= len(Z_PIECES) - 2)
        for i, (first, count) in enumerate(Z_PIECES):
            second_product(1, first, count, (len(Z_PIECES) + i) % 8, False)

        def weighted(m, d, first, count):
            part = keep.tile([P, count], F32, name="part%d_%d_%d" % (m, d, first))
            nc.vector.tensor_tensor(
                part[:], y[m][:].indirect(entries(pos_sb[d], first, count)), gate_sb[d][:, first : first + count], MULT
            )
            return part

        def finish(m, first, count, a, b, tag):
            res = keep.tile([P, count], F32, name="res%d_%d" % (m, first), tag=tag)
            nc.vector.tensor_tensor(res[:], a, b, ADD)
            nc.sync.dma_start(out[P * m : P * (m + 1), first : first + count], res[:])

        for i, first in enumerate(range(0, V, HALF)):
            turned = bank(2 + i, HALF, "turned%d" % i)
            parts = [weighted(0, d, first, HALF) for d in range(2)]
            order = [(part, n) for part in parts for n in range(2)]
            for step, (part, n) in enumerate(order):
                nc.tensor.matmul(
                    turned[:, P * n : P * (n + 1)],
                    lhsT=part[:, P * n : P * (n + 1)],
                    rhs=ident[:],
                    is_transpose=True,
                    start=step == 0,
                    stop=step == len(order) - 1,
                )
            sums = keep.tile([P, HALF], F32, name="sums%d" % i)
            nc.scalar.copy(sums[:], turned[:])
            back = bank(4 + i, HALF, "back%d" % i)
            for n in range(2):
                nc.tensor.transpose(back[:, P * n : P * (n + 1)], sums[:, P * n : P * (n + 1)], ident[:])
            res = keep.tile([P, HALF], F32, name="res0_%d" % i)
            nc.scalar.copy(res[:], back[:])
            nc.scalar.dma_start(out[0:P, first : first + HALF], res[:])
        a1 = weighted(1, 0, 0, V)
        pending = None
        for first, count in OUT_PIECES:
            b1 = weighted(1, 1, first, count)
            if pending is not None:
                finish(*pending)
            pending = (1, first, count, a1[:, first : first + count], b1[:], "res%d" % first)
        finish(*pending)
